import numpy as np, ml_dtypes
CORES = [24,48,72,152,176,200]
N = 6
BF = ml_dtypes.bfloat16
def gentries(a):
    return np.ascontiguousarray(a.reshape(8, 16, -1).transpose(0, 2, 1)).reshape(8, -1)
def gtable(e):
    e = np.asarray(e); return np.ascontiguousarray(e.reshape(8, -1, 16).transpose(0, 2, 1)).reshape(128, -1).astype(np.int32)
L, A, B, H, RO, K = 1024, 256, 3, 1, 2, 10
def woven(rng, lens, ring):
    lens = np.asarray(lens); e = np.add.accumulate(lens); s = e - lens; ring = np.asarray(ring) & (lens > 2)
    nx = np.arange(1, L + 1); nx[e - 1] = np.where(ring, s, L)
    pv = np.arange(-1, L - 1); pv[s] = np.where(ring, e - 1, L)
    p = np.append(rng.permutation(L), L); a = np.zeros((2, L), np.int64); a[0, p[:L]] = p[nx]; a[1, p[:L]] = p[pv]
    return np.where(rng.random(L) < 0.5, a[::-1], a), p[:L]
def hills(rng, lens, p):
    lens = np.asarray(lens); k = np.repeat(np.arange(len(lens)), lens); at = np.arange(L) - (np.add.accumulate(lens) - lens)[k]; sh = (len(lens), 16)
    top = rng.random(sh) * lens[:, None]; steep = np.minimum(np.exp2(1 + 5 * rng.random(sh)) * np.power(lens.astype(np.float64), -1.0)[:, None], 0.5); high = 0.3 + 0.7 * rng.random(sh)
    v = high[k] * np.maximum(np.exp(-np.abs(at[:, None] - top[k]) * steep[k]), 0.05) * (0.5 + 0.5 * rng.random((L, 16)))
    x = np.zeros((L, 16), np.int32); x[p] = np.floor(255 * v).astype(np.int32)
    return x
def cands(rng, a):
    free = (a[0] == L) | (a[1] == L); own = np.arange(L); c = np.zeros((B + H, L), np.int64)
    for i in range(B):
        o = np.argsort(rng.random(L) + np.where(free, 0.0, 1.0) * (rng.random(L) < 0.8)); c[i, o[0::2]] = o[1::2]; c[i, o[1::2]] = o[0::2]
        u = rng.random(L); w = a[rng.integers(0, 2, L), own]
        c[i] = np.where(u < 0.15, rng.integers(0, L, L), np.where((u < 0.3) & (w < L), w, np.where((u > 0.3) & (u < 0.32), own, c[i])))
    c[B:] = rng.integers(0, A, (H, L))
    return c
def cuts(rng, n, span):
    o = np.sort(rng.permutation(span - 1)[:n - 1]) + 1
    return np.diff(np.concatenate([[0], o, [L]]))
def ends(rng, n):
    if n < 2: return np.array([1] * n + [L - n]), np.array([False] * n + [True])
    one = n % 2; h = n // 2; rest = L - one - 2 * h; o = np.sort(rng.integers(0, rest + 1, h - 1))
    lens = np.concatenate([np.ones(one, np.int64), 2 + np.diff(np.concatenate([[0], o, [rest]]))])
    return lens, np.zeros(len(lens), bool)
def common(rng, q):
    n = (3, 12, 60, 150)[(q + q // 8) % 4]
    return cuts(rng, n, int(L * (0.3 + 0.6 * rng.random()))), rng.random(n) < 0.2
def parts(rng, form, bind=None):
    M, X, C = [], [], []
    for q in range(8 * N):
        lens, ring = form(rng, q); a, p = woven(rng, lens, ring); x = hills(rng, lens, p); c = cands(rng, a)
        if bind is not None: bind(q, lens, p, x, c)
        M.append(a); X.append(x); C.append(c)
    return np.stack(M), np.stack(X), np.stack(C)
def levels(rng, M, X, C, share, hold=False, bump=0, still=None, fix=None):
    th, left = [], []; still = np.zeros(8 * N, bool) if still is None else still; fix = np.full((8 * N, RO), -1) if fix is None else fix
    for t in range(RO):
        m, E, W = walks(M, X); v = np.sort(np.where(m < L, W, 0), axis=1); c = np.add.reduce((m < L).astype(np.int64), axis=1)
        i = np.clip(2 * L - 1 - np.floor(share * c).astype(np.int64), 0, 2 * L - 1)
        b = np.clip(v[np.arange(8 * N), i] + rng.integers(0, bump + 1, 8 * N), 1, 8160)
        if hold and t == 0: b = np.full(8 * N, 8192)
        b = np.where(still, 8192, b); b = np.where(fix[:, t] >= 0, fix[:, t], b); th.append(b)
        m = np.where((m < L) & (W >= b[:, None]), L, m); left.append(np.add.reduce(((m[:, :L] == L) | (m[:, L:] == L)).astype(np.int64), axis=1))
        if t < RO - 1: M, X = turn(C, X, E, m)
    assert np.all(left[-1][still] <= np.minimum(A, left[0][still]) * 3 // 4)
    return np.stack(th, axis=1)
def pack(M, X, C, th):
    return {"nb": np.stack([gtable(a) for a in M.reshape(N, 8, -1)]), "cd": np.stack([gtable(a) for a in C.reshape(N, 8, -1)]),
            "th": np.repeat(th, 16, axis=0).reshape(N, 128, RO).astype(np.int32), "x0": np.ascontiguousarray(X.transpose(0, 2, 1)).reshape(N, 128, L).astype(np.float32).astype(BF)}
def setup_inputs(rng):
    M, X, C = parts(rng, common)
    return pack(M, X, C, levels(rng, M, X, C, 0.02 + 0.28 * rng.random(8 * N)))
def setup_inputs_room(rng):
    q = np.arange(8 * N); still = (q % 8 == 1) | (q % 8 == 4) | (q % 8 == 6); fall = (q % 8 == 7) & (q // 8 % (H + 1) < H)
    size = np.where(still, np.array([A, A + 1, A // 2])[(q // 8 + q % 8) % 3], np.array([A, A + 1, A - 1, 0, 1, 2 * A, A, A + 1])[(q + q // 8) % 8])
    size = np.where(q % 8 == 7, np.where(fall, A - 16, 2 * A), size); fix = np.where((q % 8 == 7)[:, None], rng.integers(8161, 8193, (8 * N, RO)), -1)
    def bind(q, lens, p, x, c):
        e = np.add.accumulate(lens); s = e - lens
        if q % 8 == 7:
            u, w = p[e - 1], p[s]; x[w] = 255
            if fall[q]:
                f = np.roll(w, -1); x[u] = 255; c[:B, u] = f; c[:B, f] = u
                if q // 8 >= N // 2: c[:B, u[:4]] = u[:4]; c[:B, f[:4]] = f[:4]
            else:
                c[:B, u] = u; c[:B, w] = p[s + 1]; c[B:, u] = rng.integers(0, A - 16, (H, len(u))); c[B:, u[0]] = A - 17; c[B:, w] = rng.integers(A - 16, A, (H, len(w)))
            return
        if not still[q]: return
        k = np.nonzero(lens > 1)[0]; k = k[:len(k) // 2 * 2]
        i, j = k[0::2], k[1::2]; u, v, w = p[e[i] - 1], p[e[j] - 1], p[s[i]]
        big = np.maximum.reduceat(x[p], s, axis=0); x[u] = np.maximum(big[i], big[j]); x[v] = x[u]
        c[:B, u] = v; c[:B, v] = u; c[:B, w] = w
        for d in range(1, H + 1):
            top = min(A, int(size[(q - 8 * d) % (8 * N)])); c[B + d - 1, w] = rng.integers(top * 3 // 4, top, len(w)); c[B + d - 1, w[0]] = top - 1
    M, X, C = parts(rng, lambda rng, q: ends(rng, int(size[q])), bind)
    return pack(M, X, C, levels(rng, M, X, C, 0.02 + 0.28 * rng.random(8 * N), hold=True, still=still, fix=fix))
def setup_inputs_ties(rng):
    M, X, C = parts(rng, common); X = X // 64 * 85
    return pack(M, X, C, levels(rng, M, X, C, 0.02 + 0.28 * rng.random(8 * N), bump=1))
def setup_inputs_rings(rng):
    def form(rng, q):
        i = (q + q // 8) % 8; k = L // 3
        if i == 0: lens = [L]
        elif i == 1: lens = [1, L - 1]
        elif i == 2: lens = [L]
        elif i == 3: lens = [3] * k + [L - 3 * k] * int(L > 3 * k)
        elif i == 4: lens = [2] * (L // 2)
        elif i == 5: lens = cuts(rng, 40, L // 2)
        elif i == 6: lens = [1] * L
        else: lens = cuts(rng, 60, L // 2)
        return np.array(lens), (rng.random(len(lens)) < 0.5) if i == 7 else np.full(len(lens), i != 2)
    M, X, C = parts(rng, form); X = rng.integers(0, 16, (8 * N, L, 16)).astype(np.int32)
    X[np.arange(8 * N)[:, None], rng.integers(0, L, (8 * N, 16)), np.arange(16)] = rng.integers(100, 256, (8 * N, 16))
    fix = np.full((8 * N, RO), -1)
    for q in range(8 * N):
        i = (q + q // 8) % 8
        if q // 8 % 2 == 0 and i == 4:
            X[q] = np.where(np.arange(L) < np.minimum(M[q, 0], M[q, 1]), 255, 0)[:, None]; fix[q] = (8161, 8192)[q // 16 % 2]
        if q // 8 % 2 == 0 and i == 6:
            o = rng.permutation(L); u, v = o[0::2], o[1::2]; c = C[q]; c[:B, u] = v; c[:B, v] = v; c[B - 1, v] = u
            x = rng.integers(64, 256, (L, 16)); x[v] = x[u]; X[q] = x; fix[q] = 8192
    return pack(M, X, C, levels(rng, M, X, C, 0.02 + 0.28 * rng.random(8 * N), bump=1, fix=fix))
def setup_inputs_alike(rng):
    M, X, C = parts(rng, common); own = np.arange(L); fix = np.full((8 * N, RO), -1)
    for q in range(8 * N):
        g = q % 8
        if g < 2: C[q, :B] = rng.choice(np.array([0, L - 1, L // 2, 3]), (B, L))
        if g == 2: w = M[q][rng.integers(0, 2, (B, L)), own]; C[q, :B] = np.where(w < L, w, own)
        if g in (3, 4): C[q, 1:B] = C[q, 0]
        if g == 5: X[q] = 77
        if g == 5 and q // 8 % 2 == 0: fix[q, 0] = 0
        if g % 2 == 0: C[q, B:] = rng.choice(np.array([0, 1, A - 1]), (H, L))
    return pack(M, X, C, levels(rng, M, X, C, 0.02 + 0.28 * rng.random(8 * N), fix=fix))
def setup_inputs_spread(rng):
    M, X, C = parts(rng, common)
    v = 256 * rng.random((8 * N, L, 16)) * np.exp2(-rng.integers(0, 9, (8 * N, L, 1))) * (rng.random((8 * N, L, 1)) > 0.0625)
    X = np.minimum(np.floor(v), 255).astype(np.int32)
    return pack(M, X, C, levels(rng, M, X, C, rng.random(8 * N) ** 3))
def check_inputs(d):
    bad = []; G = np.arange(8 * N)[:, None]; own = np.arange(L)
    M = np.stack([gentries(a) for a in d["nb"]]).astype(np.int64).reshape(8 * N, 2, L); C = np.stack([gentries(a) for a in d["cd"]]).astype(np.int64).reshape(8 * N, B + H, L)
    if np.min(M) < 0 or np.max(M) > L: bad.append("range of nb")
    else:
        if np.any(M == own): bad.append("nb: a layer linked to itself")
        if np.any((M[:, 0] == M[:, 1]) & (M[:, 0] < L)): bad.append("nb: both slots name one layer")
        P = np.concatenate([M, np.full((8 * N, 2, 1), L)], axis=2)
        for s in range(2):
            m = M[:, s]
            if not np.all((m == L) | (P[:, 0][G, m] == own) | (P[:, 1][G, m] == own)): bad.append("nb: a link of one side only, slot " + str(s))
    if np.min(C) < 0 or np.max(C[:, :B]) > L - 1 or np.max(C[:, B:]) > A - 1: bad.append("range of cd")
    t = d["th"].reshape(8 * N, 16, RO)
    if np.min(t) < 0 or np.max(t) > 8192: bad.append("range of th")
    if np.any(t != t[:, :1]): bad.append("th: rows of a group that differ")
    v = d["x0"].astype(np.float32)
    if not np.all((v >= 0) & (v <= 255) & (v == np.floor(v))): bad.append("x0: whole numbers from 0 to 255")
    return bad
def walks(M, X):
    Q = len(M); G = np.arange(Q)[:, None]; m = M.reshape(Q, 2 * L)
    came = np.concatenate([M[:, 0], np.full((Q, 1), L)], axis=1)[G, m] == np.tile(np.arange(L), 2)
    back = np.where(m < L, np.where(came, m, L + m), 2 * L)
    step = np.concatenate([np.where(m < L, np.where(came, L + m, m), 2 * L), np.full((Q, 1), 2 * L)], axis=1)
    E = np.concatenate([X, X, np.zeros((Q, 1, 16), X.dtype)], axis=1); P = step[G, step]
    for k in range(K):
        E = np.maximum(E, E[G, P]); P = P[G, P]
    D = np.add.reduce(np.abs(E - E[G, step]), axis=2)
    return m, E, D[:, :2 * L] + D[G, back]
def turn(C, X, E, m):
    Q = len(X); G = np.arange(Q)[:, None]; own = np.arange(L); M = m.reshape(Q, 2, L)
    X = (X + np.abs(E[:, :L] - E[:, L:2 * L])) >> 1
    free = (M[:, 0] == L) | (M[:, 1] == L); place = np.add.accumulate(free.astype(np.int64), axis=1) - 1
    q, n = np.nonzero(free & (place < A)); S = np.zeros((Q, A, 16), X.dtype); S[q, place[q, n]] = X[q, n]
    S = S.reshape(N, 8, A, 16)
    come = [np.roll(S, d, axis=0).reshape(Q, A, 16)[G, C[:, B + d - 1]] for d in range(1, H + 1)]
    far = []
    for i in range(B):
        c = C[:, i]; ok = free[G, c] & (c != own) & (c != M[:, 0]) & (c != M[:, 1])
        far.append(np.where(ok, np.add.reduce(np.abs(X - X[G, c]), axis=2), 2 ** 20))
    for v in come: far.append(np.add.reduce(np.abs(X - v), axis=2))
    pick = np.argmin(np.stack(far, axis=1), axis=1)
    to = np.where(free & (pick < B), np.take_along_axis(C, pick[:, None, :], 1)[:, 0], L)
    both = (to < L) & (np.concatenate([to, np.full((Q, 1), L)], axis=1)[G, to] == own); low = M[:, 0] == L
    M = np.stack([np.where(both & low, to, M[:, 0]), np.where(both & ~low, to, M[:, 1])], axis=1)
    for d, v in enumerate(come): X = np.where((free & (pick == B + d))[:, :, None], (X + v) >> 1, X)
    return M, X
def reference(nb, cd, th, x0):
    M = np.stack([gentries(a) for a in nb]).astype(np.int64).reshape(8 * N, 2, L); C = np.stack([gentries(a) for a in cd]).astype(np.int64).reshape(8 * N, B + H, L)
    X = np.ascontiguousarray(x0.astype(np.float32).reshape(8 * N, 16, L).transpose(0, 2, 1)).astype(np.int32); t = th.astype(np.int64).reshape(8 * N, 16, RO)[:, 0]
    for rnd in range(RO):
        m, E, W = walks(M, X)
        M, X = turn(C, X, E, np.where((m < L) & (W >= t[:, rnd:rnd + 1]), L, m))
    return {"yn": np.stack([gtable(a) for a in M.reshape(N, 8, 2 * L)]).astype(np.float32), "yx": np.ascontiguousarray(X.transpose(0, 2, 1)).reshape(N, 128, L).astype(np.float32).astype(BF)}

from concourse.mybir import AluOpType, ActivationFunctionType

L, NS, END, ROOM, LEVELS, ROUNDS = 1024, 2048, 2048, 256, 10, 2
MAGIC = 12582912.0
FAR = 65536.0
POISON = 4096.0


def _pool(items):
    at, out = 0, {}
    for name, n in items:
        out[name] = (at, n)
        at += (n + 15) // 16 * 16
    return out, at


WF, NF = _pool([("m", 128), ("m1", 80), ("ml", 128), ("thr", 128), ("step", 128), ("back", 128), ("thf", 2), ("thw", 128), ("t", 128),
                ("a", 128), ("b", 128), ("c", 128), ("e", 128), ("s1", 128), ("s2", 128), ("cf", 192), ("v", 192), ("mm", 64), ("k0", 64),
                ("best", 64), ("bm", 64), ("kf", 64), ("nn0", 64), ("frac", 128), ("naf", 64), ("w", 64), ("lq", 64), ("D", 64),
                ("d2", 128), ("km", 1), ("wc", 1), ("wp", 1), ("wq", 1), ("endc", 1), ("n0", 64), ("ntab", 64), ("pm", 16), ("j16", 16)])
WI, NI = _pool([("nb", 128), ("cd", 256), ("th", 2), ("ia", 8), ("sh", 8), ("kmi", 1), ("k2", 1), ("i1", 128), ("i2", 128), ("bi", 64),
                ("i3", 64), ("ci", 64)])
WB, NB = _pool([("t1", 128), ("t2", 128), ("lo", 128), ("hi", 128), ("f", 64), ("inc", 64), ("own", 192), ("eq", 192),
                ("Bw", 144), ("Bc", 144), ("Bp", 144), ("Bq", 144), ("ident", 128), ("negI", 128), ("halfI", 128), ("farI", 128),
                ("nfarI", 128), ("Blk", 128), ("TmB", 128), ("quart", 128), ("ones", 512)])
WU, NU = _pool([("oc", 256), ("ocame", 128), ("O0", 128), ("O1", 128), ("opos", 128), ("ostep", 128), ("oback", 128),
                ("osc", 64), ("oq", 64), ("omk", 64), ("ojn", 64), ("ofin", 64), ("olow", 64), ("oci", 64)])
POOLS = {"wf": WF, "wi": WI, "wb": WB, "wu": WU}
WIDE = NS + 16

SCRATCH = {
    "wf": ("sbuf", [128, NF], "float32"), "wi": ("sbuf", [128, NI], "int32"),
    "wb": ("sbuf", [128, NB], "bfloat16"), "wu": ("sbuf", [128, NU], "uint16"),
    "X2": ("sbuf", [128, WIDE], "bfloat16"), "Ea": ("sbuf", [128, WIDE], "bfloat16"), "Eb": ("sbuf", [128, WIDE], "bfloat16"),
    "T0": ("sbuf", [128, WIDE], "bfloat16"), "Ta": ("sbuf", [128, WIDE], "bfloat16"), "Tb": ("sbuf", [128, WIDE], "bfloat16"),
    "Ed": ("sbuf", [128, NS], "bfloat16"), "Xp": ("sbuf", [128, 3 * L], "bfloat16"), "Xq": ("sbuf", [128, L], "bfloat16"),
    "blk": ("sbuf", [128, NS], "bfloat16"),
    "land0": ("sbuf", [128, ROOM], "bfloat16"), "land1": ("sbuf", [128, ROOM], "bfloat16"),
    "mk": ("sbuf", [128, L], "float32"), "iot": ("sbuf", [128, L], "float32"),
    "psA": ("psum", [128, 512], "float32"), "psB": ("psum", [128, 512], "float32"),
    "psC": ("psum", [128, 512], "float32"), "psD": ("psum", [128, 512], "float32"),
    "psd": ("psum", [128, 1024], "float32"), "pss": ("psum", [128, 1024], "float32"),
}
NDMA = 20
SEMAPHORES = ["sV", "sS", "sP", "sG", "arr0", "arr1", "loc0", "loc1", "dup0", "dup1", "dup2", "dup3"] + ["d%d" % i for i in range(NDMA)]
Alu, Act = AluOpType, ActivationFunctionType
ENGINES = 8


def _first(topo, src, dst, n):
    m = 0
    for e in topo.engines(src, dst)[:n]:
        m |= 1 << e
    return m


def _relay(topo, T, src, dst):
    if topo.may_write(src, dst):
        return None
    can = [c for c in topo.cores_of(src) if T.rank_of(c) is None and topo.may_write(c, dst)]
    near = [c for c in can if topo.die(c) == topo.die(src)]
    return (near or can)[0]


def rank_program(g, core, T, topo):
    cores = list(T.cores)
    n = len(cores)
    rank = T.rank_of(core)
    if rank is None:
        for q in range(n):
            src, dst = cores[q], cores[(q + 1) % n]
            if _relay(topo, T, src, dst) == core:
                rid, pid = topo.addr(dst, core)
                for t in range(ROUNDS):
                    g.wait_ge(T.sem["arr%d" % t], ENGINES)
                    g.remote_dma(T["land%d" % t][:], T["land%d" % t][:], T.sem["arr%d" % t], T.sem["loc%d" % t], pid, rid,
                                 _first(topo, core, dst, ENGINES))
                for t in range(ROUNDS):
                    g.wait_ge(T.sem["loc%d" % t], ENGINES)
        return
    dst = cores[(rank + 1) % n]
    hop = _relay(topo, T, core, dst)
    _rank(g, core, T, topo, dst if hop is None else hop)


def _rank(g, core, T, topo, to_core):
    Q = {"V": g.vector, "S": g.scalar, "P": g.tensor, "G": g, "Y": g.sync}
    count = {}
    known = {q: {} for q in Q}
    seen = {}
    uses = {}
    ndma = [0]

    def need(q, sem, val):
        if known[q].get(sem, 0) >= val:
            return
        Q[q].wait_ge(T.sem[sem], val)
        for s, v in seen[(sem, val)].items():
            if known[q].get(s, 0) < v:
                known[q][s] = v

    def issue(q, who, sem, inc, emit, reads, writes):
        want = {}
        for regs, wr in ((reads, False), (writes, True)):
            for name, lo, hi in regs:
                ps = name.startswith("ps")
                for ulo, uhi, uwr, uwho, usem, uval in uses.get(name, []):
                    if ps and uwho != who:
                        hit = ulo // 512 <= (hi - 1) // 512 and lo // 512 <= (uhi - 1) // 512
                    elif ps and who == "P":
                        hit = False
                    else:
                        hit = (wr or uwr) and ulo < hi and lo < uhi
                    if hit and want.get(usem, 0) < uval:
                        want[usem] = uval
        for s, v in want.items():
            need(q, s, v)
        ins = emit()
        count[sem] = count.get(sem, 0) + inc
        if ins is not None:
            ins.then_inc(T.sem[sem], inc)
        snap = dict(known[q])
        snap[sem] = count[sem]
        seen[(sem, count[sem])] = snap
        for regs, wr in ((reads, False), (writes, True)):
            for name, lo, hi in regs:
                old = uses.get(name, [])
                if wr:
                    old = [u for u in old if not (lo <= u[0] and u[1] <= hi)]
                uses[name] = old + [(lo, hi, wr, who, sem, count[sem])]

    def A(name, lo=0, hi=None, step=1, rows=None):
        for pool, tab in POOLS.items():
            if name in tab:
                base, width = tab[name]
                name, lo, hi = pool, base + lo, base + (width if hi is None else hi)
                break
        t = T[name]
        if hi is None:
            hi = t.shape[1]
        r = slice(0, 128) if rows is None else rows
        return (t[r, lo:hi] if step == 1 else t[r, lo:hi:step], [(name, lo, hi)], [])

    def C(name, c, w=512, at=0):
        return A(name, at + c * w, at + c * w + w)

    def ind(win, off):
        return (win[0].indirect(off[0]), win[1], off[1])

    def rd(*ops):
        out = []
        for o in ops:
            if isinstance(o, tuple):
                out += o[1] + o[2]
        return out

    def val(o):
        return o[0] if isinstance(o, tuple) else o

    def comp(q, emit, out, *ins):
        issue(q, q, "s" + q, 1, emit, rd(*ins) + out[2], out[1])

    def tt(out, a, b, op):
        comp("V", lambda: g.vector.tensor_tensor(out[0], a[0], b[0], op), out, a, b)

    def ts(out, a, s1, op0, s2=None, op1=None):
        if op1 is None:
            comp("V", lambda: g.vector.tensor_scalar(out[0], a[0], val(s1), None, op0), out, a, s1)
        else:
            comp("V", lambda: g.vector.tensor_scalar(out[0], a[0], val(s1), val(s2), op0, op1), out, a, s1, s2)

    def cp(out, a):
        comp("V", lambda: g.vector.tensor_copy(out[0], a[0]), out, a)

    def fill(out, c):
        comp("V", lambda: g.vector.memset(out[0], c), out)

    def act(out, a, func, bias=0.0, scale=1.0):
        comp("S", lambda: g.scalar.activation(out[0], a[0], func, val(bias), scale), out, a, bias)

    def lin(out, a, scale, bias):
        act(out, a, Act.Identity, bias, scale)

    def const(out, c):
        w = out[1][0][2] - out[1][0][1]
        lin(out, A("iot", 0, w), 0.0, c)

    def pick(out, a):
        comp("S", lambda: g.scalar.activation(out[0], a[0], Act.Copy), out, a)

    def mm(out, terms, start=True, stop=True):
        def emit():
            for i, (lhs, rhs) in enumerate(terms):
                ins = g.tensor.matmul(out[0], lhs[0], rhs[0], start and i == 0, stop and i == len(terms) - 1)
            return ins
        comp("P", emit, out, *[o for pair in terms for o in pair])

    def wrap(out, mat, name, lo, start=True, stop=True):
        mm(out, [(A(mat, 15 - r, 143 - r), A(name, lo + r, lo + L, 16)) for r in range(16)], start, stop)

    def dma(q, out, src, sem=None):
        if sem is None:
            sem = "d%d" % ndma[0]
            ndma[0] += 1
        issue(q, sem, sem, 16, lambda: Q[q].dma_start(out[0], src[0]), src[1], out[1])

    def spread(q, row, src):
        dma(q, (T.T0[row:128:16, 0:NS], [("T0row%d" % row, 0, 1)], []), src)

    T0all = [("T0row%d" % r, 0, 1) for r in range(4)]

    def sel(out, src, pattern, cmp, base, mult):
        comp("G", lambda: g.affine_select(out[0], src[0], pattern, cmp, 0.0, base, mult), out, src)

    def gcopy(out, src):
        sel(out, src, [[0, 512]], Alu.is_ge, 0, 0)

    def iota(out, pattern, base, mult, small=True):
        if small:
            comp("G", lambda: g.iota(out[0], pattern, base, mult, allow_small_or_imprecise_dtypes=True), out)
        else:
            comp("G", lambda: g.iota(out[0], pattern, base, mult), out)

    def hbm(ap):
        return (ap, [], [])

    H = [(0, 64), (64, 128)]
    PS = [A("psA", 0, 64), A("psB", 0, 64)]
    X1 = A("Xp", L, NS)

    dma("Y", A("nb"), hbm(T.nb[:]))
    dma("S", A("cd"), hbm(T.cd[:]))
    dma("Y", A("th"), hbm(T.th[:]))
    dma("S", A("X2", 0, L), hbm(T.x0[:]))
    dma("Y", A("X2", L, NS), hbm(T.x0[:]))
    dma("Y", A("Xq"), hbm(T.x0[:]))
    iota(A("ia"), [[-16, 8]], 0, 1, False)
    iota(A("iot"), [[1, L]], 1, 0)
    iota(A("n0"), [[16, 64]], 0, 0)
    iota(A("j16"), [[1, 16]], 0, 0)
    fill((T.T0[:, :], [("T0", 0, WIDE)] + T0all, []), 0.0)
    fill(A("Bc"), 0.0)
    fill(A("m1"), 0.0)
    ts(A("sh"), A("ia"), 4, Alu.arith_shift_right)
    ts(A("kmi"), A("ia", 0, 1), 15, Alu.bitwise_and)
    ts(A("wc"), A("kmi"), 16.0, Alu.add)
    ts(A("k2"), A("kmi"), 1, Alu.arith_shift_right)
    cp(A("km"), A("kmi"))
    ts(A("endc"), A("kmi"), 1.0, Alu.is_equal, float(END), Alu.mult)
    ts(A("Bc", 15, 143, 16), A("sh"), 0.0, Alu.is_equal, A("wc"), Alu.mult)
    ts(A("wp"), A("k2"), 1.0, Alu.is_equal, 1023.0, Alu.mult)
    ts(A("wq"), A("k2"), 0.0, Alu.is_equal)
    for nm in ("Bp", "Bw", "Bq"):
        const(A(nm), 0.0)
    lin(A("wp"), A("wp"), 1.0, 1.0)
    for nm in ("T0", "Ta", "Tb"):
        lin(A(nm, END, END + 1), A("endc"), 1.0, 0.0)
    for nm in ("X2", "Ea", "Eb"):
        const(A(nm, END, END + 1), 0.0)
    for nm, c in (("ident", 1.0), ("negI", -1.0), ("halfI", 0.5), ("farI", FAR), ("nfarI", -FAR), ("frac", 1.0 / 4096)):
        const(A(nm), c)
        sel(A(nm), A(nm), [[-1, 128]], Alu.is_equal, 0, 1)
    const(A("Blk"), 1.0)
    const(A("TmB"), -1.0)
    sel(A("Blk"), A("Blk"), [[-16, 8], [0, 16]], Alu.is_ge, 0, 1)
    sel(A("TmB"), A("TmB"), [[-1, 128]], Alu.is_gt, 0, 1)
    sel(A("Blk"), A("Blk"), [[16, 8], [0, 16]], Alu.is_ge, 15, -1)
    sel(A("TmB"), A("TmB"), [[16, 8], [0, 16]], Alu.is_ge, 15, -1)
    const(A("quart"), -0.25)
    const(A("ones"), 1.0)
    const(A("Xp", NS, 3 * L), POISON)
    const(A("blk", 0, ROOM), 0.0)
    lin(A("n0"), A("n0"), 1.0, A("km"))
    lin(A("nn0"), A("n0"), -1.0, 0.0)
    lin(A("ntab"), A("n0"), 1.0, L + 1 - FAR)

    ts(A("i1"), A("nb"), 4, Alu.arith_shift_right)
    ts(A("m1", 0, 64), A("nb", 0, 64), 1.0, Alu.add)
    cp(A("ocame"), A("i1"))
    for h, (a, b) in enumerate(H):
        tt(C("Ea", h, L), ind(A("m1"), A("ocame", a, b)), A("iot"), Alu.is_equal)
        wrap(A("psA", a, b), "Bc", "Ea", h * L)
    ts(A("i2"), A("nb"), 15, Alu.bitwise_and)
    cp(A("hi"), A("nb"))
    ts(A("thr"), A("nb"), float(L), Alu.is_lt, 32.0, Alu.mult)
    ts(A("ml"), A("i2"), 16.0, Alu.add)
    tt(A("lo"), A("nb"), A("hi"), Alu.subtract)
    spread("Y", 1, A("hi"))
    spread("Y", 0, A("lo"))
    tt(A("t1"), A("psA", 0, 128), A("ml"), Alu.is_equal)
    tt(A("t2"), A("psA", 0, 128), A("thr"), Alu.is_ge)
    spread("Y", 2, A("t1"))
    spread("S", 3, A("t2"))
    tt(A("a"), A("t1"), A("t2"), Alu.add)
    ts(A("Bp", 15, 143, 16), A("sh"), 0.0, Alu.is_equal, A("wp"), Alu.mult)
    ts(A("a"), A("a"), float(L), Alu.mult)
    tt(A("step"), A("a"), A("nb"), Alu.add)

    for t in range(ROUNDS):
        last = t == ROUNDS - 1
        land = "land%d" % t
        Bp = "Bp" if t == 0 else "Bq"
        ts(A("i2"), A("step"), -7.5, Alu.add, 1.0 / 16, Alu.mult)
        ts(A("a"), A("step"), 128.0, Alu.mult)
        ts(A("b"), A("i2"), -2047.0, Alu.mult, float(END - 128 * END), Alu.max)
        tt(A("a"), A("a"), A("b"), Alu.add)
        cp(A("opos"), A("a"))
        if t > 0:
            ts(A("e"), A("step"), float(L), Alu.is_ge, float(L), Alu.mult)
        win0 = (T.T0[:, 0:WIDE], [("T0", 0, WIDE)] + T0all, [])
        for h in range(2):
            cp(C("Ta", 2 * h), ind(win0, C("opos", 2 * h, 32)))
            pick(C("Ta", 2 * h + 1), ind(win0, C("opos", 2 * h + 1, 32)))
            wrap(PS[h], Bp, "Ta", h * L)
        if t == 0:
            cp(A("m"), A("nb"))
            cp(A("cf"), A("cd", 0, 192))
        else:
            tt(A("m"), A("step"), A("e"), Alu.subtract)
        lin(A("s1"), A("m"), 2.0, float(L))
        cp(A("O0", 0, 64), PS[0])

        tabs, E = ["Ta", "Tb"], "X2"
        for k in range(LEVELS):
            O, On, Pin, Pout, Eout = "O%d" % (k % 2), "O%d" % ((k + 1) % 2), tabs[k % 2], tabs[(k + 1) % 2], ("Ea", "Eb")[k % 2]
            more = k < LEVELS - 1
            for p, c in enumerate((1, 0, 3, 2) if k % 2 else (0, 1, 2, 3)):
                if p == 0 and more:
                    pick(C(Pout, 0, L), ind(A(Pin), A(O, 0, 64)))
                    wrap(PS[0], Bp, Pout, 0)
                tt(C(Eout, c), ind(A(E), C(O, c, 32)), C("Xq", c % 2) if k == 0 else C("Ed", c), Alu.max)
                if p % 2 == 0:
                    dma("Y", C("Ed", c), C(Eout, c), "dup%d" % (p + k % 2))
                else:
                    gcopy(C("Ed", c), C(Eout, c))
                if p == (1 if k == 0 else 0):
                    cp(A(O, 64, 128), PS[1])
                    if more:
                        pick(C(Pout, 1, L), ind(A(Pin), A(O, 64, 128)))
                        wrap(PS[1], Bp, Pout, L)
                if p == 0 and k == 0:
                    cp(A("ostep"), A("step"))
                if p == 2 and more:
                    cp(A(On, 0, 64), PS[0])
                if not more:
                    if p == 0 and t == 0:
                        for i in range(3):
                            mm(C("psD", i, 64), [(A("frac"), C("cf", i, 64)), (A("frac"), A("nn0"))])
                            lin(C("v", i, 64), C("cf", i, 64), 1.0, float(i * L))
                        act(A("psD", 0, 192), A("psD", 0, 192), Act.Abs)
                        act(A("own"), A("psD", 0, 192), Act.Relu, FAR, -FAR * 4096)
                    if p == 0:
                        for h in range(2):
                            mm(C("pss", h), [(A("halfI"), C("X2", h)), (A("quart", rows=slice(0, 1)), A("ones", rows=slice(0, 1)))], True, False)
                    mm(C("psd", c % 2), [(A("ident" if c < 2 else "negI"), C(Eout, c))], c < 2, c >= 2)
            E = Eout

        for c in range(4):
            tt(C("Ea", c), ind(A("Eb"), C("ostep", c, 32)), C("Ed", c), Alu.subtract)
            if c < 2:
                act(C("Xq", 1 - c), C("psd", 1 - c), Act.Abs)
                mm(C("pss", 1 - c), [(A("halfI"), C("Xq", 1 - c))], False, True)
            act(C("Ta", c), C("Ea", c), Act.Abs)
            if c % 2:
                wrap(PS[c // 2], "Bw", "Ta", (c // 2) * L, True, False)
            if t == 0 and c == 0:
                ts(A("Bw", 15, 143, 16), A("sh"), 0.0, Alu.is_equal)
        tt(A("back"), A("s1"), A("step"), Alu.subtract)
        if t == 0:
            cp(A("thf"), A("th"))
        cp(A("oback"), A("back"))
        ts(A("thw"), A("m"), float(L), Alu.is_lt, A("thf", t, t + 1), Alu.mult)
        for h in range(2):
            cp(C("Tb", 2 * h), ind(A("Ta", 0, NS), C("oback", 2 * h, 32)))
            pick(C("Tb", 2 * h + 1), ind(A("Ta", 0, NS), C("oback", 2 * h + 1, 32)))
            wrap(PS[h], "Bw", "Tb", h * L, False, True)
        ts(X1, A("pss"), MAGIC, Alu.add, MAGIC, Alu.subtract)
        if t == 0:
            cp(A("oc"), A("cd"))

        tt(A("t", 0, 64), PS[0], A("thw", 0, 64), Alu.is_ge)
        tt(A("t", 64, 128), PS[1], A("thw", 64, 128), Alu.is_ge)
        tt(A("f"), A("t", 0, 64), A("t", 64, 128), Alu.max)
        comp("V", lambda: g.vector.tensor_tensor_scan(A("inc")[0], A("ones", 0, 64)[0], A("f")[0], 0.0, Alu.mult, Alu.add), A("inc"), A("ones", 0, 64), A("f"))
        lin(A("s2", 0, 64), A("f"), -float(L), 0.0)
        mm(A("psD", 0, 64), [(A("nfarI"), A("f")), (A("TmB"), A("f")), (A("Blk"), A("inc"))])
        for h in range(2):
            mm(C("psd", h), [(A("negI"), C("Xp", h, 512, L))], True, False)
            mm(C("pss", h), [(A("ident"), C("Xp", h, 512, L))], True, False)
        tt(A("lq"), A("s2", 0, 64), A("ntab"), Alu.add)
        tt(A("a", 0, 64), A("psD", 0, 64), A("lq"), Alu.min)
        ts(A("oq"), A("lq"), FAR - 1, Alu.add)
        ts(A("osc"), A("a", 0, 64), FAR - 1, Alu.add)
        pick(A("Xq"), ind(A("Xp", L, 3 * L), A("oq")))
        cp(ind(A("blk"), A("osc")), X1)
        rid, pid = topo.addr(to_core, core)

        def send():
            g.remote_dma(T[land][:], A("blk", 0, ROOM)[0], T.sem["arr%d" % t], T.sem["loc%d" % t], pid, rid, _first(topo, core, to_core, ENGINES))
        issue("G", "loc%d" % t, "loc%d" % t, ENGINES, send, A("blk", 0, ROOM)[1], [])
        count["arr%d" % t] = ENGINES
        seen[("arr%d" % t, ENGINES)] = {"arr%d" % t: ENGINES}
        uses[land] = [(0, ROOM, True, "far", "arr%d" % t, ENGINES)]

        for h in range(2):
            pick(C("Eb", h), ind(A("Xq"), C("oc", h, 32)))
            mm(C("psd", h), [(A("ident"), C("Eb", h))], False, True)
        for h in range(2):
            act(C("Tb", h), C("psd", h), Act.Abs)
        lin(A("s1"), A("t"), float(L), 0.0)
        lin(A("kf"), A("f"), -FAR, FAR - 0.75)
        if not last:
            lin(A("s2"), A("t"), float(END), 0.0)
        keys = A("psC", 0, 192)
        mm(keys, [(A("frac"), A("v")), (A("ident"), A("own"))], True, False)
        wrap(C("psC", 0, 64), "Bw", "Tb", 0, False, False)
        for h in range(2):
            mm(C("psd", h), [(A("negI"), C("Xp", h, 512, L))], True, False)
        for c in range(4):
            tt(C("Ea", c), ind(A("Xq"), C("oc", c, 32, 64)), C("Xp", c % 2, 512, L), Alu.subtract)
            act(C("Ta", c), C("Ea", c), Act.Abs)
            if c == 1:
                wrap(C("psC", 1, 64), "Bw", "Ta", 0, False, False)
        wrap(C("psC", 2, 64), "Bw", "Ta", L, False, False)
        if not last:
            cp(A("olow"), A("t", 0, 64))
            pick(A("Eb", 0, L), ind(A("iot", 0, 16), A("olow")))
        tt(A("m"), A("m"), A("s1"), Alu.max)
        tt(A("mm"), A("m", 0, 64), A("m", 64, 128), Alu.min)
        for i in range(3):
            tt(C("eq", i, 64), C("cf", i, 64), A("mm"), Alu.is_equal)
        mm(keys, [(A("farI"), A("eq"))], False, True)
        if t == 0:
            ts(A("pm"), A("j16"), A("km"), Alu.is_equal, 2.0, Alu.mult)
            tt(A("step"), A("step"), A("s2"), Alu.max)
            ts(A("pm"), A("pm"), -1.0, Alu.add)

        for h in range(2):
            pick(C("Eb", h, 512, L), ind(A(land), C("oc", h, 32, 192)))
            mm(C("psd", h), [(A("ident"), C("Eb", h, 512, L))], False, True)
        for h in range(2):
            act(C("Tb", h, 512, L), C("psd", h), Act.Abs)
        mm(C("pss", 0), [(A("ident"), C("Eb", 0, 512, L))], False, True)
        wrap(PS[1], "Bw", "Tb", L)
        mm(C("pss", 1), [(A("ident"), C("Eb", 1, 512, L))], False, True)

        cp(A("k0"), C("psC", 0, 64))
        tt(A("best"), C("psC", 1, 64), A("k0"), Alu.min)
        tt(A("best"), C("psC", 2, 64), A("best"), Alu.min)
        ts(A("bi"), A("best"), 4096.0, Alu.mult, 16777215.0, Alu.min)
        ts(A("i3"), A("bi"), 15, Alu.bitwise_and)
        ts(A("i1", 0, 64), A("bi"), L - 1, Alu.bitwise_and, 4, Alu.arith_shift_right)
        ts(A("ci"), A("bi"), L - 1, Alu.bitwise_and)
        cp(A("omk"), A("i3"))
        cp(A("ojn"), A("i1", 0, 64))
        if not last:
            cp(A("oci"), A("ci"))
        tt(A("mk"), ind(A("pm"), A("omk")), A("iot"), Alu.mult)
        ts(A("c", 0, 64), A("ci"), 1.0, Alu.add)
        tt(A("bm"), A("best"), A("kf"), Alu.add)
        if not last:
            pick(A("Ea", 0, L), ind(A("Eb", 0, L), A("oci")))
            wrap(PS[0], "Bw", "Ea", 0)
            sel(A("blk", 0, ROOM), A("Xp", NS, NS + ROOM), [[0, ROOM]], Alu.is_gt, 0, 0)
        for h in range(2):
            lin(C("pss", h), C("pss", h), 0.4995, MAGIC)
            lin(C("Xp", h), C("pss", h), 1.0, -MAGIC)

        tt(A("naf"), PS[1], A("bm"), Alu.is_ge)
        tt(A("w"), A("naf"), A("c", 0, 64), Alu.mult)

        def final_x():
            ts(A("e", 0, 64), A("naf"), float(L), Alu.mult, FAR - 1, Alu.add)
            tt(A("e", 0, 64), A("e", 0, 64), A("lq"), Alu.add)
            cp(A("ofin"), A("e", 0, 64))
            for h in range(2):
                pick(C("X2", h), ind(A("Xp", 0, NS), C("ofin", h, 32)))
                if last:
                    dma("Y" if h == 0 else "S", hbm(T.yx[:, 512 * h:512 * h + 512]), C("X2", h))
                else:
                    gcopy(C("X2", 2 + h), C("X2", h))
                    dma("Y", C("Xq", h), C("X2", h))
        if last:
            final_x()
        tt(A("Ea", L, NS), ind(A("w"), A("ojn")), A("mk"), Alu.is_equal)
        won = A("psD", 64, 128)
        wrap(won, "Bw", "Ea", L)
        if last:
            ts(A("D"), A("ci"), -float(L), Alu.add)
            base = "m"
        else:
            ts(A("s1", 0, 64), PS[0], L / 16.0, Alu.mult, -float(L + END), Alu.add)
            tt(A("D"), A("s1", 0, 64), A("ci"), Alu.add)
            base = "step"
        tt(A("D"), A("D"), A("naf"), Alu.mult)
        tt(A("d2", 0, 64), A("D"), A("t", 0, 64), Alu.mult)
        tt(A("d2", 64, 128), A("D"), A("d2", 0, 64), Alu.subtract)
        for a, b in H:
            tt(A("a", a, b), won, A("d2", a, b), Alu.mult)
        tt(A(base), A(base), A("a"), Alu.add)
        if last:
            dma("Y", hbm(T.yn[:]), A("m"))
            break
        cp(A("hi"), A("step"))
        spread("S", 1, A("hi"))
        tt(A("lo"), A("step"), A("hi"), Alu.subtract)
        spread("Y", 0, A("lo"))
        final_x()
        ts(A("Bq", 15, 143, 16), A("sh"), 0.0, Alu.is_equal, A("wq"), Alu.mult)

    for sem, v in count.items():
        need("G", sem, v)
